import numpy as np
import ml_dtypes


def mxq(x, axis, fmt="e4m3"):
    dtype, down = {"e4m3": (ml_dtypes.float8_e4m3fn, 7), "e5m2": (ml_dtypes.float8_e5m2, 14)}[fmt]
    v = np.moveaxis(np.asarray(x, np.float32).astype(ml_dtypes.bfloat16).astype(np.float64), axis, -1)
    blocks = v.reshape(v.shape[:-1] + (-1, 32))
    amax = np.abs(blocks).max(-1, keepdims=True)
    byte = np.maximum(np.where(amax > 0, np.frexp(amax)[1] - 1 + 127, 0) - down, 1)
    scale = np.exp2(byte - 127.0)
    codes = (blocks / scale).astype(np.float32).astype(dtype).astype(np.float64)
    return np.moveaxis((codes * scale).reshape(v.shape), -1, axis)


WIDE = False


def mx_kscale(k):
    if not WIDE:
        return np.ones(k)
    levels = np.array([30, -30])
    if k % 512:
        return np.exp2(np.random.permutation(np.resize(levels, k // 32))).repeat(32)
    a = np.empty((k // 512, 16))
    for p in range(k // 512):
        a[p, :8] = np.random.permutation(np.resize(levels, 8))
        for g in range(8):
            far = levels[np.abs(levels - a[p, g]) >= 10]
            a[p, g + 8] = far[np.random.randint(len(far))]
    return np.exp2(a.ravel()).repeat(32)


def f64(x):
    return np.asarray(x).astype(np.float64)


def striped(idx):
    return np.tile(np.asarray(idx).reshape(-1, 16).T, (8, 1)).astype(np.uint16)


def unstriped(offs):
    return offs[:16].T.reshape(-1).astype(np.int64)


E2M1 = np.array([0.0, 0.5, 1.0, 1.5, 2.0, 3.0, 4.0, 6.0, -0.0, -0.5, -1.0, -1.5, -2.0, -3.0, -4.0, -6.0])


def pack_weight(w, fmt):
    k, n = w.shape
    w = f64(np.asarray(w, np.float32).astype(ml_dtypes.bfloat16)).reshape(k // 32, 32, n)
    amax = np.abs(w).max(1)
    if fmt in ("e4m3", "e5m2"):
        byte = np.frexp(amax)[1] - 1 + 127 - (7 if fmt == "e4m3" else 14)
    else:
        mant, ex = np.frexp(amax / 6.0)
        byte = np.where(mant > 0.5, ex, ex - 1) + 127
    byte = np.clip(np.where(amax > 0, byte, 1), 1, 254)
    scaled = (w * np.exp2(127.0 - byte)[:, None, :]).reshape(k, n).astype(np.float32)
    by_word = np.ascontiguousarray(scaled.reshape(k // 512, 128, 4, n).transpose(0, 1, 3, 2))
    if fmt in ("e4m3", "e5m2"):
        words = by_word.astype(ml_dtypes.float8_e4m3fn if fmt == "e4m3" else ml_dtypes.float8_e5m2).view(np.uint8)
    else:
        c = by_word.astype(ml_dtypes.float4_e2m1fn).view(np.uint8) & 0xF
        words = (c[..., 0::2] | (c[..., 1::2] << 4)).reshape(k // 512, 128, 2 * n)
    return np.ascontiguousarray(words), np.ascontiguousarray(byte.astype(np.uint8).reshape(k // 512, 16, n))


def unpack_weight(words, scales, fmt):
    g, _, n = scales.shape
    words = np.ascontiguousarray(words).reshape(g, 128, n, -1)
    if fmt in ("e4m3", "e5m2"):
        vals = words.view(ml_dtypes.float8_e4m3fn if fmt == "e4m3" else ml_dtypes.float8_e5m2).astype(np.float64)
    else:
        nib = np.empty((g, 128, n, 4), np.uint8)
        nib[..., 0::2] = words & 0xF
        nib[..., 1::2] = words >> 4
        vals = E2M1[nib]
    vals = vals * np.repeat(np.exp2(scales.astype(np.float64) - 127.0), 8, axis=1)[..., None]
    return vals.transpose(0, 1, 3, 2).reshape(g * 512, n)


K, Q, T, J, N = 512, 128, 1024, 256, 256


def setup_inputs():
    n = np.random.standard_normal
    idx = np.random.permutation(T)[:J]
    fk = mx_kscale(K)
    pha = np.random.uniform(0.0, 2.0 * np.pi, (Q, 1))
    phb = np.random.uniform(0.0, 2.0 * np.pi, (Q, 1))
    wp = pack_weight(n((K, N)) * 1 / np.sqrt(K) / fk[:, None], "e5m2")
    return {
        "ra": (0.9 * n((Q, T))).astype(np.float32),
        "ia": (0.9 * n((Q, T))).astype(np.float32),
        "rb": (0.9 * n((Q, T))).astype(np.float32),
        "ib": (0.9 * n((Q, T))).astype(np.float32),
        "ca": (np.cos(pha) * fk[::4, None]).astype(np.float32),
        "na": (-np.sin(pha) * fk[::4, None]).astype(np.float32),
        "sa": (np.sin(pha) * fk[::4, None]).astype(np.float32),
        "cb": (np.cos(phb) * fk[::4, None]).astype(np.float32),
        "nb": (-np.sin(phb) * fk[::4, None]).astype(np.float32),
        "sb": (np.sin(phb) * fk[::4, None]).astype(np.float32),
        "w_words": wp[0],
        "w_scales": wp[1],
        "offs": striped(idx),
    }


def reference(ra, ia, rb, ib, ca, na, sa, cb, nb, sb, w_words, w_scales, offs):
    idx = unstriped(offs)
    wu = unpack_weight(w_words, w_scales, "e5m2")
    v0 = f64(ra)[:, idx] * f64(ca)
    v1 = f64(ia)[:, idx] * f64(na)
    v2 = f64(rb)[:, idx] * f64(cb)
    v3 = f64(ib)[:, idx] * f64(nb)
    zr = np.stack([v0, v1, v2, v3], axis=1).reshape(K, J)
    u0 = f64(ra)[:, idx] * f64(sa)
    u1 = f64(ia)[:, idx] * f64(ca)
    u2 = f64(rb)[:, idx] * f64(sb)
    u3 = f64(ib)[:, idx] * f64(cb)
    zi = np.stack([u0, u1, u2, u3], axis=1).reshape(K, J)
    zrq = mxq(zr, 0, "e4m3")
    p = wu.T @ zrq
    ziq = mxq(zi, 0, "e4m3")
    d = wu.T @ ziq
    y = np.square(p) + np.square(d)
    return y

@@ -1,0 +1,147 @@
+from contextlib import ExitStack
+
+import concourse.mybir as mybir
+
+K, Q, T, J, N = 512, 128, 1024, 256, 256
+FLOPS = 2 * 2 * K * N * J
+
+F32 = mybir.dt.float32
+BF16 = mybir.dt.bfloat16
+I32 = mybir.dt.int32
+U32 = mybir.dt.uint32
+U16 = mybir.dt.uint16
+U8 = mybir.dt.uint8
+E4M3X4 = mybir.dt.float8_e4m3fn_x4
+E5M2X4 = mybir.dt.float8_e5m2_x4
+ACT = mybir.ActivationFunctionType
+ADD = mybir.AluOpType.add
+MULT = mybir.AluOpType.mult
+
+P = 128
+PACK = 4
+HEAD = 192
+TAIL = J - HEAD
+
+
+def tile_list_beams_kernel(tc, ra, ia, rb, ib, ca, na, sa, cb, nb, sb, w_words, w_scales, offs, out):
+    nc = tc.nc
+    with ExitStack() as ctx:
+        keep = ctx.enter_context(tc.tile_pool(name="keep", bufs=1))
+        psum = ctx.enter_context(tc.psum_pool(name="psum", bufs=1))
+
+        def load_column(queue, name, src):
+            col = keep.tile([P, 1], F32, name=name)
+            queue.dma_start(out=col[:], in_=src)
+            return col
+
+        def load_record(name, src):
+            rec = keep.tile([P, T], F32, name=name)
+            nc.sync.dma_start(out=rec[:], in_=src)
+            return rec
+
+        ca_t = load_column(nc.scalar, "ca_t", ca)
+        ra_t = load_record("ra_t", ra)
+        sa_t = load_column(nc.scalar, "sa_t", sa)
+        offsets = keep.tile([P, J // 16], U16, name="offsets")
+        nc.sync.dma_start(offsets[:], offs)
+        na_t = load_column(nc.scalar, "na_t", na)
+        ia_t = load_record("ia_t", ia)
+        cb_t = load_column(nc.sync, "cb_t", cb)
+        rb_t = load_record("rb_t", rb)
+        sb_t = load_column(nc.sync, "sb_t", sb)
+        nb_t = load_column(nc.sync, "nb_t", nb)
+        ib_t = load_record("ib_t", ib)
+        records = (ra_t, ia_t, rb_t, ib_t)
+        real_factors = (ca_t, na_t, cb_t, nb_t)
+        imag_factors = (sa_t, ca_t, sb_t, cb_t)
+
+        warm_in = keep.tile([P, 1], F32, name="warm_in")
+        warm_out = keep.tile([P, 1], F32, name="warm_out")
+        nc.vector.memset(warm_in[:], 0.0)
+        nc.scalar.activation(out=warm_out[:], in_=warm_in[:], func=ACT.Square)
+
+        w_rows = keep.tile([4, 4, N // 4], I32, name="w_rows")
+        nc.gpsimd.dma_start(out=w_rows[:], in_=w_scales[0].bitcast(I32).rearrange("(q r) n -> r q n", r=4))
+        w_codes = keep.tile([P, N], I32, name="w_codes", align_bytes=64)
+        nc.sync.dma_start(out=w_codes[:], in_=w_words[0].rearrange("p n t -> p (n t)").bitcast(I32))
+        w_plane = keep.tile([P, N], U8, name="w_plane", align_bytes=64)
+        nc.vector.memset(w_plane[:].bitcast(I32), 0)
+        for q in range(4):
+            nc.vector.tensor_copy(out=w_plane[32 * q : 32 * q + 4, :].bitcast(I32), in_=w_rows[:, q, :])
+
+        z_codes = keep.tile([P, 2 * J], U32, name="z_codes", align_bytes=64)
+        z_plane = keep.tile([P, 2 * J], U8, name="z_plane", align_bytes=64)
+
+        def fetch(z, slot, factor, j0, width):
+            nc.scalar.activation(
+                out=z[:, slot : PACK * width : PACK],
+                in_=records[slot][:].indirect(offsets[:, j0 // 16 : (j0 + width) // 16]),
+                func=ACT.Copy,
+                scale=factor[:],
+            )
+
+        def quantise(z, c0, width, word0):
+            nc.vector.quantize_mx(
+                out=z_codes[:, word0 : word0 + width].bitcast(E4M3X4),
+                scales=z_plane[:, word0 : word0 + width],
+                in_=z[:, PACK * c0 : PACK * (c0 + width)],
+            )
+
+        def multiply(bank, col0, half, word0, width):
+            beams = slice(half * P, (half + 1) * P)
+            nc.tensor.matmul_mx(
+                out=bank[:, col0 : col0 + width],
+                lhsT=w_codes[:, beams].bitcast(E5M2X4),
+                lhsT_scale=w_plane[:, beams],
+                rhs=z_codes[:, word0 : word0 + width].bitcast(E4M3X4),
+                rhs_scale=z_plane[:, word0 : word0 + width],
+                start=True,
+                stop=True,
+            )
+
+        def power(sq, name, half, j0, width):
+            y = keep.tile([P, width], F32, name=name + "_y")
+            nc.vector.tensor_tensor(out=y[:], in0=sq[:, 0:width], in1=sq[:, width : 2 * width], op=ADD)
+            nc.sync.dma_start(out=out[half * P : (half + 1) * P, j0 : j0 + width], in_=y[:])
+
+        zr = keep.tile([P, PACK * HEAD], BF16, name="zr_head", tag="zr", align_bytes=64)
+        zi = keep.tile([P, PACK * HEAD], BF16, name="zi_head", tag="zi", align_bytes=64)
+        for slot in range(PACK):
+            fetch(zr, slot, real_factors[slot], 0, HEAD)
+            fetch(zi, slot, imag_factors[slot], 0, HEAD)
+        quantise(zr, 0, 128, 0)
+        quantise(zr, 128, 64, 128)
+        early_bank = psum.tile([P, 2 * 128], F32, name="early_bank")
+        head_banks = [psum.tile([P, 256], F32, name="head_bank%d" % half) for half in range(2)]
+        for half in range(2):
+            multiply(early_bank, 128 * half, half, 0, 128)
+        quantise(zi, 0, 128, HEAD)
+        quantise(zi, 128, 64, HEAD + 128)
+        for half in range(2):
+            multiply(head_banks[half], 0, half, 128, 256)
+        head_sq = [keep.tile([P, 2 * HEAD], F32, name="head_sq%d" % half) for half in range(2)]
+        early_sums = keep.tile([P, 2 * 128], F32, name="early_sums")
+        nc.vector.tensor_copy(out=early_sums[:], in_=early_bank[:])
+        for half in range(2):
+            cols = slice(128 * half, 128 * (half + 1))
+            nc.vector.tensor_tensor(out=head_sq[half][:, 0:128], in0=early_bank[:, cols], in1=early_sums[:, cols], op=MULT)
+
+        zr = keep.tile([P, PACK * TAIL], BF16, name="zr_tail", tag="zr", align_bytes=64)
+        zi = keep.tile([P, PACK * TAIL], BF16, name="zi_tail", tag="zi", align_bytes=64)
+        for slot in range(PACK):
+            fetch(zr, slot, real_factors[slot], HEAD, TAIL)
+        for slot in range(PACK):
+            fetch(zi, slot, imag_factors[slot], HEAD, TAIL)
+        quantise(zr, 0, TAIL, 2 * HEAD)
+        quantise(zi, 0, TAIL, 2 * HEAD + TAIL)
+        tail_banks = [psum.tile([P, 2 * TAIL], F32, name="tail_bank%d" % half) for half in range(2)]
+        for half in range(2):
+            multiply(tail_banks[half], 0, half, 2 * HEAD, 2 * TAIL)
+
+        for half in range(2):
+            nc.scalar.activation(out=head_sq[half][:, 128 : 2 * HEAD], in_=head_banks[half][:], func=ACT.Square)
+            power(head_sq[half], "head%d" % half, half, 0, HEAD)
+        for half in range(2):
+            tail_sq = keep.tile([P, 2 * TAIL], F32, name="tail_sq%d" % half)
+            nc.scalar.activation(out=tail_sq[:], in_=tail_banks[half][:], func=ACT.Square)
+            power(tail_sq, "tail%d" % half, half, HEAD, TAIL)

@@ -55,11 +55,6 @@ def tile_list_beams_kernel(tc, ra, ia, rb, ib, ca, na, sa, cb, nb, sb, w_words, 
         real_factors = (ca_t, na_t, cb_t, nb_t)
         imag_factors = (sa_t, ca_t, sb_t, cb_t)
 
-        warm_in = keep.tile([P, 1], F32, name="warm_in")
-        warm_out = keep.tile([P, 1], F32, name="warm_out")
-        nc.vector.memset(warm_in[:], 0.0)
-        nc.scalar.activation(out=warm_out[:], in_=warm_in[:], func=ACT.Square)
-
         w_rows = keep.tile([4, 4, N // 4], I32, name="w_rows")
         nc.gpsimd.dma_start(out=w_rows[:], in_=w_scales[0].bitcast(I32).rearrange("(q r) n -> r q n", r=4))
         w_codes = keep.tile([P, N], I32, name="w_codes", align_bytes=64)

@@ -39,21 +39,25 @@ def tile_list_beams_kernel(tc, ra, ia, rb, ib, ca, na, sa, cb, nb, sb, w_words, 
             nc.sync.dma_start(out=rec[:], in_=src)
             return rec
 
-        ca_t = load_column(nc.scalar, "ca_t", ca)
         ra_t = load_record("ra_t", ra)
-        sa_t = load_column(nc.scalar, "sa_t", sa)
+        ca_t = load_column(nc.scalar, "ca_t", ca)
         offsets = keep.tile([P, J // 16], U16, name="offsets")
         nc.sync.dma_start(offsets[:], offs)
-        na_t = load_column(nc.scalar, "na_t", na)
+        sa_t = load_column(nc.sync, "sa_t", sa)
         ia_t = load_record("ia_t", ia)
+        na_t = load_column(nc.sync, "na_t", na)
         cb_t = load_column(nc.sync, "cb_t", cb)
         rb_t = load_record("rb_t", rb)
         sb_t = load_column(nc.sync, "sb_t", sb)
-        nb_t = load_column(nc.sync, "nb_t", nb)
         ib_t = load_record("ib_t", ib)
+        nb_t = load_column(nc.sync, "nb_t", nb)
         records = (ra_t, ia_t, rb_t, ib_t)
-        real_factors = (ca_t, na_t, cb_t, nb_t)
         imag_factors = (sa_t, ca_t, sb_t, cb_t)
+
+        warm_in = keep.tile([P, 1], F32, name="warm_in")
+        warm_out = keep.tile([P, 1], F32, name="warm_out")
+        nc.vector.memset(warm_in[:], 0.0)
+        nc.scalar.activation(out=warm_out[:], in_=warm_in[:], func=ACT.Square)
 
         w_rows = keep.tile([4, 4, N // 4], I32, name="w_rows")
         nc.gpsimd.dma_start(out=w_rows[:], in_=w_scales[0].bitcast(I32).rearrange("(q r) n -> r q n", r=4))
@@ -67,9 +71,9 @@ def tile_list_beams_kernel(tc, ra, ia, rb, ib, ca, na, sa, cb, nb, sb, w_words, 
         z_codes = keep.tile([P, 2 * J], U32, name="z_codes", align_bytes=64)
         z_plane = keep.tile([P, 2 * J], U8, name="z_plane", align_bytes=64)
 
-        def fetch(z, slot, factor, j0, width):
+        def fetch(z, c0, slot, factor, j0, width):
             nc.scalar.activation(
-                out=z[:, slot : PACK * width : PACK],
+                out=z[:, PACK * c0 + slot : PACK * (c0 + width) : PACK],
                 in_=records[slot][:].indirect(offsets[:, j0 // 16 : (j0 + width) // 16]),
                 func=ACT.Copy,
                 scale=factor[:],
@@ -99,21 +103,28 @@ def tile_list_beams_kernel(tc, ra, ia, rb, ib, ca, na, sa, cb, nb, sb, w_words, 
             nc.vector.tensor_tensor(out=y[:], in0=sq[:, 0:width], in1=sq[:, width : 2 * width], op=ADD)
             nc.sync.dma_start(out=out[half * P : (half + 1) * P, j0 : j0 + width], in_=y[:])
 
-        zr = keep.tile([P, PACK * HEAD], BF16, name="zr_head", tag="zr", align_bytes=64)
+        zr = keep.tile([P, PACK * J], BF16, name="zr", align_bytes=64)
         zi = keep.tile([P, PACK * HEAD], BF16, name="zi_head", tag="zi", align_bytes=64)
-        for slot in range(PACK):
-            fetch(zr, slot, real_factors[slot], 0, HEAD)
-            fetch(zi, slot, imag_factors[slot], 0, HEAD)
-        quantise(zr, 0, 128, 0)
-        quantise(zr, 128, 64, 128)
+        fetch(zr, 0, 0, ca_t, 0, J)
+        fetch(zi, 0, 0, sa_t, 0, HEAD)
+        fetch(zi, 0, 1, ca_t, 0, HEAD)
+        fetch(zr, 0, 1, na_t, 0, J)
+        fetch(zr, 0, 2, cb_t, 0, J)
+        fetch(zi, 0, 2, sb_t, 0, HEAD)
+        fetch(zi, 0, 3, cb_t, 0, HEAD)
+        fetch(zr, 0, 3, nb_t, 0, HEAD)
+        fetch(zr, HEAD, 3, nb_t, HEAD, TAIL)
+        quantise(zi, 0, 128, 0)
+        quantise(zi, 128, 64, 128)
         early_bank = psum.tile([P, 2 * 128], F32, name="early_bank")
         head_banks = [psum.tile([P, 256], F32, name="head_bank%d" % half) for half in range(2)]
         for half in range(2):
             multiply(early_bank, 128 * half, half, 0, 128)
-        quantise(zi, 0, 128, HEAD)
-        quantise(zi, 128, 64, HEAD + 128)
+        quantise(zr, 0, 128, HEAD)
+        quantise(zr, 128, 64, HEAD + 128)
         for half in range(2):
             multiply(head_banks[half], 0, half, 128, 256)
+        quantise(zr, HEAD, TAIL, 2 * HEAD)
         head_sq = [keep.tile([P, 2 * HEAD], F32, name="head_sq%d" % half) for half in range(2)]
         early_sums = keep.tile([P, 2 * 128], F32, name="early_sums")
         nc.vector.tensor_copy(out=early_sums[:], in_=early_bank[:])
@@ -121,13 +132,9 @@ def tile_list_beams_kernel(tc, ra, ia, rb, ib, ca, na, sa, cb, nb, sb, w_words, 
             cols = slice(128 * half, 128 * (half + 1))
             nc.vector.tensor_tensor(out=head_sq[half][:, 0:128], in0=early_bank[:, cols], in1=early_sums[:, cols], op=MULT)
 
-        zr = keep.tile([P, PACK * TAIL], BF16, name="zr_tail", tag="zr", align_bytes=64)
         zi = keep.tile([P, PACK * TAIL], BF16, name="zi_tail", tag="zi", align_bytes=64)
         for slot in range(PACK):
-            fetch(zr, slot, real_factors[slot], HEAD, TAIL)
-        for slot in range(PACK):
-            fetch(zi, slot, imag_factors[slot], HEAD, TAIL)
-        quantise(zr, 0, TAIL, 2 * HEAD)
+            fetch(zi, 0, slot, imag_factors[slot], HEAD, TAIL)
         quantise(zi, 0, TAIL, 2 * HEAD + TAIL)
         tail_banks = [psum.tile([P, 2 * TAIL], F32, name="tail_bank%d" % half) for half in range(2)]
         for half in range(2):

@@ -49,6 +49,8 @@ def tile_list_beams_kernel(tc, ra, ia, rb, ib, ca, na, sa, cb, nb, sb, w_words, 
         cb_t = load_column(nc.sync, "cb_t", cb)
         rb_t = load_record("rb_t", rb)
         sb_t = load_column(nc.sync, "sb_t", sb)
+        w_rows = keep.tile([4, 4, N // 4], I32, name="w_rows")
+        nc.sync.dma_start(out=w_rows[:], in_=w_scales[0].bitcast(I32).rearrange("(q r) n -> r q n", r=4))
         ib_t = load_record("ib_t", ib)
         nb_t = load_column(nc.sync, "nb_t", nb)
         records = (ra_t, ia_t, rb_t, ib_t)
@@ -59,8 +61,6 @@ def tile_list_beams_kernel(tc, ra, ia, rb, ib, ca, na, sa, cb, nb, sb, w_words, 
         nc.vector.memset(warm_in[:], 0.0)
         nc.scalar.activation(out=warm_out[:], in_=warm_in[:], func=ACT.Square)
 
-        w_rows = keep.tile([4, 4, N // 4], I32, name="w_rows")
-        nc.gpsimd.dma_start(out=w_rows[:], in_=w_scales[0].bitcast(I32).rearrange("(q r) n -> r q n", r=4))
         w_codes = keep.tile([P, N], I32, name="w_codes", align_bytes=64)
         nc.sync.dma_start(out=w_codes[:], in_=w_words[0].rearrange("p n t -> p (n t)").bitcast(I32))
         w_plane = keep.tile([P, N], U8, name="w_plane", align_bytes=64)
@@ -143,7 +143,9 @@ def tile_list_beams_kernel(tc, ra, ia, rb, ib, ca, na, sa, cb, nb, sb, w_words, 
         for half in range(2):
             nc.scalar.activation(out=head_sq[half][:, 128 : 2 * HEAD], in_=head_banks[half][:], func=ACT.Square)
             power(head_sq[half], "head%d" % half, half, 0, HEAD)
+        tail_y = keep.tile([P, 2, TAIL], F32, name="tail_y")
         for half in range(2):
             tail_sq = keep.tile([P, 2 * TAIL], F32, name="tail_sq%d" % half)
             nc.scalar.activation(out=tail_sq[:], in_=tail_banks[half][:], func=ACT.Square)
-            power(tail_sq, "tail%d" % half, half, HEAD, TAIL)
+            nc.vector.tensor_tensor(out=tail_y[:, half, :], in0=tail_sq[:, 0:TAIL], in1=tail_sq[:, TAIL : 2 * TAIL], op=ADD)
+        nc.sync.dma_start(out=out[:, HEAD:J].rearrange("(h p) j -> p h j", p=P), in_=tail_y[:])

from contextlib import ExitStack

import concourse.mybir as mybir

K, Q, T, J, N = 512, 128, 1024, 256, 256
FLOPS = 2 * 2 * K * N * J

F32 = mybir.dt.float32
BF16 = mybir.dt.bfloat16
I32 = mybir.dt.int32
U32 = mybir.dt.uint32
U16 = mybir.dt.uint16
U8 = mybir.dt.uint8
E4M3X4 = mybir.dt.float8_e4m3fn_x4
E5M2X4 = mybir.dt.float8_e5m2_x4
ACT = mybir.ActivationFunctionType
ADD = mybir.AluOpType.add
MULT = mybir.AluOpType.mult

P = 128
PACK = 4
HEAD = 192
TAIL = J - HEAD


def tile_list_beams_kernel(tc, ra, ia, rb, ib, ca, na, sa, cb, nb, sb, w_words, w_scales, offs, out):
    nc = tc.nc
    with ExitStack() as ctx:
        keep = ctx.enter_context(tc.tile_pool(name="keep", bufs=1))
        psum = ctx.enter_context(tc.psum_pool(name="psum", bufs=1))

        def load_column(queue, name, src):
            col = keep.tile([P, 1], F32, name=name)
            queue.dma_start(out=col[:], in_=src)
            return col

        def load_record(name, src):
            rec = keep.tile([P, T], F32, name=name)
            nc.sync.dma_start(out=rec[:], in_=src)
            return rec

        ra_t = load_record("ra_t", ra)
        ca_t = load_column(nc.scalar, "ca_t", ca)
        offsets = keep.tile([P, J // 16], U16, name="offsets")
        nc.sync.dma_start(offsets[:], offs)
        sa_t = load_column(nc.sync, "sa_t", sa)
        ia_t = load_record("ia_t", ia)
        na_t = load_column(nc.sync, "na_t", na)
        cb_t = load_column(nc.sync, "cb_t", cb)
        rb_t = load_record("rb_t", rb)
        sb_t = load_column(nc.sync, "sb_t", sb)
        w_rows = keep.tile([4, 4, N // 4], I32, name="w_rows")
        nc.sync.dma_start(out=w_rows[:], in_=w_scales[0].bitcast(I32).rearrange("(q r) n -> r q n", r=4))
        ib_t = load_record("ib_t", ib)
        nb_t = load_column(nc.sync, "nb_t", nb)
        records = (ra_t, ia_t, rb_t, ib_t)
        imag_factors = (sa_t, ca_t, sb_t, cb_t)

        warm_in = keep.tile([P, 1], F32, name="warm_in")
        warm_out = keep.tile([P, 1], F32, name="warm_out")
        nc.vector.memset(warm_in[:], 0.0)
        nc.scalar.activation(out=warm_out[:], in_=warm_in[:], func=ACT.Square)

        w_codes = keep.tile([P, N], I32, name="w_codes", align_bytes=64)
        nc.sync.dma_start(out=w_codes[:], in_=w_words[0].rearrange("p n t -> p (n t)").bitcast(I32))
        w_plane = keep.tile([P, N], U8, name="w_plane", align_bytes=64)
        nc.vector.memset(w_plane[:].bitcast(I32), 0)
        for q in range(4):
            nc.vector.tensor_copy(out=w_plane[32 * q : 32 * q + 4, :].bitcast(I32), in_=w_rows[:, q, :])

        z_codes = keep.tile([P, 2 * J], U32, name="z_codes", align_bytes=64)
        z_plane = keep.tile([P, 2 * J], U8, name="z_plane", align_bytes=64)

        def fetch(z, c0, slot, factor, j0, width):
            nc.scalar.activation(
                out=z[:, PACK * c0 + slot : PACK * (c0 + width) : PACK],
                in_=records[slot][:].indirect(offsets[:, j0 // 16 : (j0 + width) // 16]),
                func=ACT.Copy,
                scale=factor[:],
            )

        def quantise(z, c0, width, word0):
            nc.vector.quantize_mx(
                out=z_codes[:, word0 : word0 + width].bitcast(E4M3X4),
                scales=z_plane[:, word0 : word0 + width],
                in_=z[:, PACK * c0 : PACK * (c0 + width)],
            )

        def multiply(bank, col0, half, word0, width):
            beams = slice(half * P, (half + 1) * P)
            nc.tensor.matmul_mx(
                out=bank[:, col0 : col0 + width],
                lhsT=w_codes[:, beams].bitcast(E5M2X4),
                lhsT_scale=w_plane[:, beams],
                rhs=z_codes[:, word0 : word0 + width].bitcast(E4M3X4),
                rhs_scale=z_plane[:, word0 : word0 + width],
                start=True,
                stop=True,
            )

        def power(sq, name, half, j0, width):
            y = keep.tile([P, width], F32, name=name + "_y")
            nc.vector.tensor_tensor(out=y[:], in0=sq[:, 0:width], in1=sq[:, width : 2 * width], op=ADD)
            nc.sync.dma_start(out=out[half * P : (half + 1) * P, j0 : j0 + width], in_=y[:])

        zr = keep.tile([P, PACK * J], BF16, name="zr", align_bytes=64)
        zi = keep.tile([P, PACK * HEAD], BF16, name="zi_head", tag="zi", align_bytes=64)
        fetch(zr, 0, 0, ca_t, 0, J)
        fetch(zi, 0, 0, sa_t, 0, HEAD)
        fetch(zi, 0, 1, ca_t, 0, HEAD)
        fetch(zr, 0, 1, na_t, 0, J)
        fetch(zr, 0, 2, cb_t, 0, J)
        fetch(zi, 0, 2, sb_t, 0, HEAD)
        fetch(zi, 0, 3, cb_t, 0, HEAD)
        fetch(zr, 0, 3, nb_t, 0, HEAD)
        fetch(zr, HEAD, 3, nb_t, HEAD, TAIL)
        quantise(zi, 0, 128, 0)
        quantise(zi, 128, 64, 128)
        early_bank = psum.tile([P, 2 * 128], F32, name="early_bank")
        head_banks = [psum.tile([P, 256], F32, name="head_bank%d" % half) for half in range(2)]
        for half in range(2):
            multiply(early_bank, 128 * half, half, 0, 128)
        quantise(zr, 0, 128, HEAD)
        quantise(zr, 128, 64, HEAD + 128)
        for half in range(2):
            multiply(head_banks[half], 0, half, 128, 256)
        quantise(zr, HEAD, TAIL, 2 * HEAD)
        head_sq = [keep.tile([P, 2 * HEAD], F32, name="head_sq%d" % half) for half in range(2)]
        early_sums = keep.tile([P, 2 * 128], F32, name="early_sums")
        nc.vector.tensor_copy(out=early_sums[:], in_=early_bank[:])
        for half in range(2):
            cols = slice(128 * half, 128 * (half + 1))
            nc.vector.tensor_tensor(out=head_sq[half][:, 0:128], in0=early_bank[:, cols], in1=early_sums[:, cols], op=MULT)

        zi = keep.tile([P, PACK * TAIL], BF16, name="zi_tail", tag="zi", align_bytes=64)
        for slot in range(PACK):
            fetch(zi, 0, slot, imag_factors[slot], HEAD, TAIL)
        quantise(zi, 0, TAIL, 2 * HEAD + TAIL)
        tail_banks = [psum.tile([P, 2 * TAIL], F32, name="tail_bank%d" % half) for half in range(2)]
        for half in range(2):
            multiply(tail_banks[half], 0, half, 2 * HEAD, 2 * TAIL)

        for half in range(2):
            nc.scalar.activation(out=head_sq[half][:, 128 : 2 * HEAD], in_=head_banks[half][:], func=ACT.Square)
            power(head_sq[half], "head%d" % half, half, 0, HEAD)
        tail_y = keep.tile([P, 2, TAIL], F32, name="tail_y")
        for half in range(2):
            tail_sq = keep.tile([P, 2 * TAIL], F32, name="tail_sq%d" % half)
            nc.scalar.activation(out=tail_sq[:], in_=tail_banks[half][:], func=ACT.Square)
            nc.vector.tensor_tensor(out=tail_y[:, half, :], in0=tail_sq[:, 0:TAIL], in1=tail_sq[:, TAIL : 2 * TAIL], op=ADD)
        nc.sync.dma_start(out=out[:, HEAD:J].rearrange("(h p) j -> p h j", p=P), in_=tail_y[:])
